import numpy as np
import ml_dtypes


def mxq(x, axis, fmt="e4m3"):
    dtype, down = {"e4m3": (ml_dtypes.float8_e4m3fn, 7), "e5m2": (ml_dtypes.float8_e5m2, 14)}[fmt]
    v = np.moveaxis(np.asarray(x, np.float32).astype(ml_dtypes.bfloat16).astype(np.float64), axis, -1)
    blocks = v.reshape(v.shape[:-1] + (-1, 32))
    amax = np.abs(blocks).max(-1, keepdims=True)
    byte = np.maximum(np.where(amax > 0, np.frexp(amax)[1] - 1 + 127, 0) - down, 1)
    scale = np.exp2(byte - 127.0)
    codes = (blocks / scale).astype(np.float32).astype(dtype).astype(np.float64)
    return np.moveaxis((codes * scale).reshape(v.shape), -1, axis)


WIDE = False


def mx_kscale(k):
    if not WIDE:
        return np.ones(k)
    levels = np.array([10, -10, 5, -5, 0])
    if k % 512:
        return np.exp2(np.random.permutation(np.resize(levels, k // 32))).repeat(32)
    a = np.empty((k // 512, 16))
    for p in range(k // 512):
        a[p, :8] = np.random.permutation(np.resize(levels, 8))
        for g in range(8):
            far = levels[np.abs(levels - a[p, g]) >= 10]
            a[p, g + 8] = far[np.random.randint(len(far))]
    return np.exp2(a.ravel()).repeat(32)


def f64(x):
    return np.asarray(x).astype(np.float64)


def striped(idx):
    return np.tile(idx.reshape(-1, 16).T, (8, 1)).astype(np.uint16)


def unstriped(offs):
    return offs[:16].T.reshape(-1).astype(np.int64)


def striped8(idx):
    return np.concatenate([x.reshape(-1, 16).T for x in idx]).astype(np.uint16)


def runs(offs, k):
    lists = np.stack([offs[16 * r : 16 * r + 16].T.reshape(-1) for r in range(8)]).astype(np.int64)
    return lists[np.arange(k) % 512 // 64]


def pack_weight(w):
    k, n = w.shape
    w = f64(np.asarray(w, np.float32).astype(ml_dtypes.bfloat16)).reshape(k // 32, 32, n)
    amax = np.abs(w).max(1)
    byte = np.clip(np.where(amax > 0, np.frexp(amax)[1] - 1 + 127 - 7, 1), 1, 254)
    scaled = (w * np.exp2(127.0 - byte)[:, None, :]).reshape(k, n).astype(np.float32)
    words = np.ascontiguousarray(scaled.reshape(k // 512, 128, 4, n).transpose(0, 1, 3, 2)).astype(ml_dtypes.float8_e4m3fn).view(np.uint8)
    return words, np.ascontiguousarray(byte.astype(np.uint8).reshape(k // 512, 16, n))


def unpack_weight(words, scales):
    g, p, n, _ = words.shape
    vals = np.ascontiguousarray(words).view(ml_dtypes.float8_e4m3fn).astype(np.float64) * np.repeat(np.exp2(scales.astype(np.float64) - 127.0), 8, axis=1)[..., None]
    return vals.transpose(0, 1, 3, 2).reshape(g * 512, n)


E2M1 = np.array([0.0, 0.5, 1.0, 1.5, 2.0, 3.0, 4.0, 6.0, -0.0, -0.5, -1.0, -1.5, -2.0, -3.0, -4.0, -6.0])


def pack_fp4(w):
    k, n = w.shape
    w = f64(np.asarray(w, np.float32).astype(ml_dtypes.bfloat16)).reshape(k // 32, 32, n)
    amax = np.abs(w).max(1)
    mant, ex = np.frexp(amax / 6.0)
    byte = np.clip(np.where(amax > 0, np.where(mant > 0.5, ex, ex - 1) + 127, 1), 1, 254)
    scaled = (w * np.exp2(127.0 - byte)[:, None, :]).reshape(k, n).astype(np.float32)
    c = np.ascontiguousarray(scaled.reshape(k // 512, 128, 4, n).transpose(0, 1, 3, 2)).astype(ml_dtypes.float4_e2m1fn).view(np.uint8) & 0xF
    words = (c[..., 0::2] | (c[..., 1::2] << 4)).reshape(k // 512, 128, 2 * n)
    return np.ascontiguousarray(words), np.ascontiguousarray(byte.astype(np.uint8).reshape(k // 512, 16, n))


def unpack_fp4(words, scales):
    g, _, n = scales.shape
    words = np.ascontiguousarray(words).reshape(g, 128, n, 2)
    nib = np.empty((g, 128, n, 4), np.uint8)
    nib[..., 0::2] = words & 0xF
    nib[..., 1::2] = words >> 4
    vals = E2M1[nib] * np.repeat(np.exp2(scales.astype(np.float64) - 127.0), 8, axis=1)[..., None]
    return vals.transpose(0, 1, 3, 2).reshape(g * 512, n)


def planes(y):
    n, m = y.shape
    v = y.astype(np.float32).astype(ml_dtypes.bfloat16).astype(np.float64).reshape(n // 32, 32, m)
    top = np.abs(v).max(1)
    byte = np.clip(np.where(top > 0, np.frexp(top)[1] - 1 + 127 - 7, 1), 1, 254)
    codes = (v * np.exp2(127.0 - byte)[:, None, :]).reshape(n, m).astype(np.float32).astype(ml_dtypes.float8_e4m3fn).view(np.uint8)
    words = codes.reshape(n // 512, 128, 4, m).transpose(0, 1, 3, 2)
    return np.ascontiguousarray(words), np.ascontiguousarray(byte.astype(np.uint8).reshape(n // 512, 16, m))


K, T, S, H, J, G = 512, 2048, 512, 512, 512, 2048


def setup_inputs():
    n = np.random.standard_normal
    s = mx_kscale(K)[:, None]
    packed_xT = pack_weight(n((K, T)) * s)
    packed_w1 = pack_fp4(n((K, H)) / np.sqrt(K) / s)
    packed_dT = pack_weight(n((K, G)) / s)
    return {
        "x_words": packed_xT[0],
        "x_scales": packed_xT[1],
        "w1_words": packed_w1[0],
        "w1_scales": packed_w1[1],
        "tab": np.random.uniform(0.4, 1.4, (H, J)).astype(np.float32),
        "gs": (np.random.uniform(0.5, 1.5, (K, 1)) * s).astype(np.float32),
        "d_words": packed_dT[0],
        "d_scales": packed_dT[1],
        "offs": striped(np.random.permutation(T)[:S]),
        "n1": striped8(np.random.randint(0, J, (8, S))),
        "n2": striped8(np.stack([np.random.permutation(S) for _ in range(8)])),
        "k1": striped8(np.random.randint(0, G, (8, H))),
        "n3": striped8(np.stack([np.random.permutation(S) for _ in range(8)])),
        "n4": striped8(np.stack([np.random.permutation(S) for _ in range(8)])),
    }


def reference(x_words, x_scales, w1_words, w1_scales, tab, gs, d_words, d_scales, offs, n1, n2, k1, n3, n4):
    d_k1 = unpack_weight(d_words, d_scales)[np.arange(K)[:, None], runs(k1, K)]
    xq = unpack_weight(x_words, x_scales)[:, unstriped(offs)]
    y = unpack_fp4(w1_words, w1_scales).T @ xq
    z = f64(gs) * (y * (f64(tab)[np.arange(H)[:, None], runs(n1, H)]) - (0.5 * (y[np.arange(H)[:, None], runs(n2, H)])))
    h = 0.0625 * ((d_k1.T @ mxq(z, 0, "e4m3")))
    out_0 = (h * (h[np.arange(H)[:, None], runs(n3, H)])) * (np.tanh(h[np.arange(H)[:, None], runs(n4, H)]))
    return (out_0,) + planes(out_0)

@@ -1,0 +1,265 @@
+from contextlib import ExitStack
+
+import concourse.mybir as mybir
+
+F32 = mybir.dt.float32
+BF16 = mybir.dt.bfloat16
+I32 = mybir.dt.int32
+U32 = mybir.dt.uint32
+U16 = mybir.dt.uint16
+U8 = mybir.dt.uint8
+FP8X4 = mybir.dt.float8_e4m3fn_x4
+FP4X4 = mybir.dt.float4_e2m1fn_x4
+ALU = mybir.AluOpType
+ACT = mybir.ActivationFunctionType
+
+P = 128
+PACK = 4
+K, T, S, H, J, G = 512, 2048, 512, 512, 512, 2048
+FLOPS = 2 * K * H * S + 2 * K * H * S
+
+Z_SLICES = ((0, 256), (256, 128), (384, 128))
+OUT_SLICES = ((0, 256), (256, 128), (384, 128))
+
+
+def tile_picked_densekindgcube_none_po_kernel(
+    tc, x_words, x_scales, w1_words, w1_scales, tab, gs, d_words, d_scales,
+    offs, n1, n2, k1, n3, n4, out_0, out_1, out_2,
+):
+    nc = tc.nc
+    with ExitStack() as ctx:
+        keep = ctx.enter_context(tc.tile_pool(name="keep", bufs=1))
+        ring = ctx.enter_context(tc.tile_pool(name="ring", bufs=3))
+        psum = ctx.enter_context(tc.psum_pool(name="psum", bufs=1))
+
+        def held(shape, dtype, name, tag=None):
+            return keep.tile(shape, dtype, name=name, tag=tag or name, align_bytes=64)
+
+        def load_list(src, name):
+            t = held([P, S // 16], U16, name)
+            nc.sync.dma_start(t[:], src)
+            return t
+
+        def cols(lst, c0, n):
+            return lst[:, c0 // 16 : (c0 + n) // 16]
+
+        xs_tab = held([P, T], U8, "xs_tab")
+        ws_raw = held([P, H], U8, "ws_raw")
+        ds_tab = held([P, G], U8, "ds_tab")
+        ds_mm = held([P, H], U8, "ds_mm")
+        zero = held([P, 1], F32, "zero")
+        half = held([P, 1], F32, "half")
+        nc.gpsimd.memset(xs_tab[:].bitcast(I32), 0)
+        nc.vector.memset(ws_raw[:].bitcast(I32), 0)
+        nc.vector.memset(ds_tab[:].bitcast(I32), 0)
+        nc.gpsimd.memset(zero[:], 0.0)
+        nc.gpsimd.memset(ds_mm[:].bitcast(I32), 0)
+
+        offs_t = load_list(offs, "offs_t")
+        for r in range(4):
+            queue = nc.scalar if r % 2 else nc.sync
+            queue.dma_start(xs_tab[r:P:32, :].bitcast(I32), x_scales[0][r:16:4, :].bitcast(I32))
+        ww_raw = held([P, 2 * H], U8, "ww_raw")
+        nc.scalar.dma_start(ww_raw[:].bitcast(I32), w1_words[0].bitcast(I32))
+        xw_tab = held([P, T], U32, "xw_tab")
+        nc.sync.dma_start(xw_tab[:].bitcast(I32), x_words[0].rearrange("p n t -> p (n t)").bitcast(I32))
+        for r in range(4):
+            queue = nc.sync if r else nc.scalar
+            queue.dma_start(ws_raw[r:P:32, :].bitcast(I32), w1_scales[0][r:16:4, :].bitcast(I32))
+        nc.scalar.activation(half[:], zero[:], ACT.Sigmoid)
+        k1_t = load_list(k1, "k1_t")
+        for b in range(2):
+            nc.sync.dma_start(ds_tab[b:P:16, :].bitcast(I32), d_scales[0][b:16:2, :].bitcast(I32))
+        gs_t = held([P, PACK], F32, "gs_t")
+        nc.sync.dma_start(gs_t[:], gs.rearrange("(p t) o -> p (t o)", t=PACK))
+        n1_t = load_list(n1, "n1_t")
+        tab_v = tab.rearrange("(p t) j -> p t j", t=PACK)
+        tab_t = [held([P, J], F32, "tab%d" % t) for t in range(PACK)]
+        nc.sync.dma_start(tab_t[0][:], tab_v[:, 0, :])
+        n2_t = load_list(n2, "n2_t")
+        for t in range(1, PACK):
+            nc.sync.dma_start(tab_t[t][:], tab_v[:, t, :])
+        dw_tab = held([P, G], U32, "dw_tab")
+        nc.sync.dma_start(dw_tab[:].bitcast(I32), d_words[0].rearrange("p n t -> p (n t)").bitcast(I32))
+        n4_t = load_list(n4, "n4_t")
+        n3_t = load_list(n3, "n3_t")
+
+        xs_g = held([P, S], U8, "xs_g")
+        nc.vector.tensor_copy(xs_g[:], xs_tab[:].indirect(offs_t[:]))
+        ww = held([P, 2 * H], U8, "ww")
+        nc.vector.tensor_copy(
+            ww[:].rearrange("p (t m b) -> p t m b", t=PACK, b=2),
+            ww_raw[:].rearrange("p (m t b) -> p t m b", t=PACK, b=2),
+        )
+        xw_g = held([P, S], U32, "xw_g")
+        nc.vector.tensor_copy(xw_g[:], xw_tab[:].indirect(offs_t[:]))
+        ws = held([P, H], U8, "ws")
+        nc.vector.tensor_copy(
+            ws[:].rearrange("p (t m) -> p t m", t=PACK), ws_raw[:].rearrange("p (m t) -> p t m", t=PACK)
+        )
+        gs_half = held([P, PACK], F32, "gs_half")
+        nc.scalar.activation(gs_half[:], gs_t[:], ACT.Copy, scale=-0.5)
+
+        y_plain, y_win = [], []
+        for t in range(PACK):
+            y_ps = psum.tile([P, S], F32, name="y_ps%d" % t)
+            nc.tensor.matmul_mx(
+                y_ps[:],
+                lhsT=ww[:, 2 * P * t : 2 * P * (t + 1)].bitcast(FP4X4),
+                lhsT_scale=ws[:, P * t : P * (t + 1)],
+                rhs=xw_g[:].bitcast(FP8X4),
+                rhs_scale=xs_g[:],
+                start=True,
+                stop=True,
+            )
+            y_plain.append(held([P, S], F32, "y_plain%d" % t))
+            y_win.append(held([P, S], F32, "y_win%d" % t))
+            nc.scalar.activation(y_plain[t][:], y_ps[:], ACT.Copy, scale=gs_t[:, t : t + 1])
+            nc.scalar.activation(y_win[t][:], y_ps[:], ACT.Copy, scale=gs_half[:, t : t + 1])
+
+        ds_g = held([P, H], U8, "ds_g")
+        nc.vector.tensor_copy(ds_g[:], ds_tab[:].indirect(k1_t[:]))
+        ds_d = held([P, H], U8, "ds_d")
+        nc.vector.tensor_copy(
+            ds_d[:].rearrange("p (t m) -> p t m", t=PACK), ds_g[:].rearrange("p (m t) -> p t m", t=PACK)
+        )
+        for c in range(4):
+            src = c % 2 + 16 * (c // 2)
+            nc.sync.dma_start(ds_mm[c:P:32, :].bitcast(I32), ds_d[src:P:32, :].bitcast(I32))
+
+        dw_g = held([P, H], U32, "dw_g")
+        dw = held([P, H], U32, "dw")
+        z_codes = held([P, S], U32, "z_codes")
+        z_scales = held([P, S], U8, "z_scales")
+        h_ps = [psum.tile([P, S], F32, name="h_ps%d" % t) for t in range(PACK)]
+        h_win = [held([P, S], F32, "h_win%d" % t) for t in range(PACK)]
+
+        h_plain = [held([P, S - Z_SLICES[-1][1]], F32, "h_plain%d" % t) for t in range(PACK)]
+
+        def interleave(copy, src, n, name):
+            dst = held([P, n * PACK], BF16, name)
+            copy(dst[:].rearrange("p (c t) -> p c t", t=PACK), src[:].rearrange("p t c -> p c t"))
+            return dst
+
+        def quantize(codes, scales, src, c0, n):
+            nc.vector.quantize_mx(codes[:, c0 : c0 + n].bitcast(FP8X4), scales[:, c0 : c0 + n], src[:])
+
+        def second_product(c0, n, last):
+            for t in range(PACK):
+                nc.tensor.matmul_mx(
+                    h_ps[t][:, c0 : c0 + n],
+                    lhsT=dw[:, P * t : P * (t + 1)].bitcast(FP8X4),
+                    lhsT_scale=ds_mm[:, P * t : P * (t + 1)],
+                    rhs=z_codes[:, c0 : c0 + n].bitcast(FP8X4),
+                    rhs_scale=z_scales[:, c0 : c0 + n],
+                    start=True,
+                    stop=True,
+                )
+                if last and t < 2:
+                    nc.vector.tensor_scalar(
+                        h_win[t][:, c0 : c0 + n], h_ps[t][:, c0 : c0 + n], 1.0 / 128, None, ALU.mult
+                    )
+                else:
+                    nc.scalar.activation(
+                        h_win[t][:, c0 : c0 + n], h_ps[t][:, c0 : c0 + n], ACT.Copy, scale=1.0 / 128
+                    )
+                if not last:
+                    nc.scalar.copy(h_plain[t][:, c0 : c0 + n], h_ps[t][:, c0 : c0 + n])
+
+        steps = [(i, t) for i in range(len(Z_SLICES)) for t in range(PACK)]
+        z = {}
+        z_bf = {}
+        prod = {}
+
+        def kind_term(i, t):
+            c0, n = Z_SLICES[i]
+            a = ring.tile([P, n], F32, name="a", align_bytes=64)
+            nc.vector.tensor_tensor(
+                a[:], tab_t[t][:].indirect(cols(n1_t, c0, n)), y_plain[t][:, c0 : c0 + n], ALU.mult
+            )
+            prod[i, t] = a
+
+        kind_term(*steps[0])
+        for k, (i, t) in enumerate(steps):
+            c0, n = Z_SLICES[i]
+            if k + 1 < len(steps):
+                kind_term(*steps[k + 1])
+            if t == 0:
+                z[i] = held([P, PACK, n], F32, "z%d" % i, tag="z_bf0" if i == 2 else None)
+            nc.vector.tensor_tensor(
+                z[i][:, t, :], y_win[t][:].indirect(cols(n2_t, c0, n)), prod[i, t][:], ALU.add
+            )
+            last = i == len(Z_SLICES) - 1
+            if t == PACK - 1:
+                copy = nc.vector.tensor_copy if last else nc.scalar.copy
+                z_bf[i] = interleave(copy, z[i], n, "z_bf%d" % i)
+                if i == 0:
+                    nc.vector.tensor_copy(dw_g[:], dw_tab[:].indirect(k1_t[:]))
+                    nc.vector.tensor_copy(
+                        dw[:].rearrange("p (t m) -> p t m", t=PACK),
+                        dw_g[:].rearrange("p (m t) -> p t m", t=PACK),
+                    )
+                if last:
+                    quantize(z_codes, z_scales, z_bf[i], c0, n)
+                    second_product(c0, n, True)
+            if t == 2 and i > 0:
+                quantize(z_codes, z_scales, z_bf[i - 1], *Z_SLICES[i - 1])
+                second_product(*Z_SLICES[i - 1], False)
+
+        out_v = out_0.rearrange("(p t) j -> p t j", t=PACK)
+        words_v = out_1[0].rearrange("p n t -> p (n t)").bitcast(I32)
+        o_codes = held([P, S], U32, "o_codes")
+        o_scales = held([P, S], U8, "o_scales")
+        steps = [(i, t) for i in range(len(OUT_SLICES)) for t in range(PACK)]
+        o = [held([P, PACK, n], F32, "o%d" % i) for i, (c0, n) in enumerate(OUT_SLICES)]
+        o_bf = {}
+        gate = {}
+
+        def first_step(i, t):
+            c0, n = OUT_SLICES[i]
+            s = ring.tile([P, n], F32, name="s", align_bytes=64)
+            nc.scalar.activation(s[:], h_win[t][:].indirect(cols(n4_t, c0, n)), ACT.Sigmoid, scale=16.0)
+            u = ring.tile([P, n], F32, name="u", align_bytes=64)
+            if i == len(OUT_SLICES) - 1:
+                nc.vector.scalar_tensor_tensor(
+                    u[:], s[:], half[:], h_ps[t][:, c0 : c0 + n], ALU.subtract, ALU.mult
+                )
+            else:
+                nc.vector.tensor_tensor(
+                    u[:], h_win[t][:].indirect(cols(n3_t, c0, n)), h_plain[t][:, c0 : c0 + n], ALU.mult
+                )
+            gate[i, t] = (s, u)
+
+        def second_step(i, t):
+            c0, n = OUT_SLICES[i]
+            s, u = gate[i, t]
+            if i == len(OUT_SLICES) - 1:
+                nc.vector.tensor_tensor(
+                    o[i][:, t, :], h_win[t][:].indirect(cols(n3_t, c0, n)), u[:], ALU.mult
+                )
+            else:
+                nc.vector.scalar_tensor_tensor(o[i][:, t, :], s[:], half[:], u[:], ALU.subtract, ALU.mult)
+
+        def planes(i):
+            c0, n = OUT_SLICES[i]
+            quantize(o_codes, o_scales, o_bf[i], c0, n)
+            nc.sync.dma_start(words_v[:, c0 : c0 + n], o_codes[:, c0 : c0 + n].bitcast(I32))
+
+        first_step(*steps[0])
+        for k, (i, t) in enumerate(steps):
+            c0, n = OUT_SLICES[i]
+            if k + 1 < len(steps):
+                first_step(*steps[k + 1])
+            second_step(i, t)
+            last = i == len(OUT_SLICES) - 1
+            if t == PACK - 1:
+                nc.sync.dma_start(out_v[:, :, c0 : c0 + n], o[i][:])
+                copy = nc.vector.tensor_copy if last else nc.scalar.copy
+                o_bf[i] = interleave(copy, o[i], n, "o_bf%d" % i)
+                if last:
+                    planes(i)
+            if t == 2 and i > 0:
+                planes(i - 1)
+        for r in range(4):
+            queue = nc.scalar if r % 2 else nc.sync
+            queue.dma_start(out_2[0][r:16:4, :].bitcast(I32), o_scales[r:P:32, :].bitcast(I32))

@@ -18,8 +18,8 @@ PACK = 4
 K, T, S, H, J, G = 512, 2048, 512, 512, 512, 2048
 FLOPS = 2 * K * H * S + 2 * K * H * S
 
-Z_SLICES = ((0, 256), (256, 128), (384, 128))
-OUT_SLICES = ((0, 256), (256, 128), (384, 128))
+HALF = S // 2
+SCALAR_SHARE = 96
 
 
 def tile_picked_densekindgcube_none_po_kernel(
@@ -29,7 +29,6 @@ def tile_picked_densekindgcube_none_po_kernel(
     nc = tc.nc
     with ExitStack() as ctx:
         keep = ctx.enter_context(tc.tile_pool(name="keep", bufs=1))
-        ring = ctx.enter_context(tc.tile_pool(name="ring", bufs=3))
         psum = ctx.enter_context(tc.psum_pool(name="psum", bufs=1))
 
         def held(shape, dtype, name, tag=None):
@@ -49,48 +48,51 @@ def tile_picked_densekindgcube_none_po_kernel(
         ds_mm = held([P, H], U8, "ds_mm")
         zero = held([P, 1], F32, "zero")
         half = held([P, 1], F32, "half")
-        nc.gpsimd.memset(xs_tab[:].bitcast(I32), 0)
+        nc.gpsimd.memset(xs_tab[:, : T // 2].bitcast(I32), 0)
+        nc.vector.memset(xs_tab[:, T // 2 :].bitcast(I32), 0)
         nc.vector.memset(ws_raw[:].bitcast(I32), 0)
         nc.vector.memset(ds_tab[:].bitcast(I32), 0)
+        tab_t = [held([P, 2 * J], F32, "tab%d" % t) for t in range(PACK)]
         nc.gpsimd.memset(zero[:], 0.0)
-        nc.gpsimd.memset(ds_mm[:].bitcast(I32), 0)
+        for t in range(PACK):
+            engine = nc.gpsimd if t % 2 else nc.vector
+            engine.memset(tab_t[t][:, J:], 0.0)
+        nc.vector.memset(ds_mm[:].bitcast(I32), 0)
 
+        ww_raw = held([P, 2 * H], U8, "ww_raw")
+        nc.scalar.dma_start(ww_raw[:].bitcast(I32), w1_words[0].bitcast(I32))
         offs_t = load_list(offs, "offs_t")
+        k1_t = load_list(k1, "k1_t")
         for r in range(4):
             queue = nc.scalar if r % 2 else nc.sync
             queue.dma_start(xs_tab[r:P:32, :].bitcast(I32), x_scales[0][r:16:4, :].bitcast(I32))
-        ww_raw = held([P, 2 * H], U8, "ww_raw")
-        nc.scalar.dma_start(ww_raw[:].bitcast(I32), w1_words[0].bitcast(I32))
         xw_tab = held([P, T], U32, "xw_tab")
         nc.sync.dma_start(xw_tab[:].bitcast(I32), x_words[0].rearrange("p n t -> p (n t)").bitcast(I32))
         for r in range(4):
-            queue = nc.sync if r else nc.scalar
-            queue.dma_start(ws_raw[r:P:32, :].bitcast(I32), w1_scales[0][r:16:4, :].bitcast(I32))
+            nc.sync.dma_start(ws_raw[r:P:32, :].bitcast(I32), w1_scales[0][r:16:4, :].bitcast(I32))
         nc.scalar.activation(half[:], zero[:], ACT.Sigmoid)
-        k1_t = load_list(k1, "k1_t")
         for b in range(2):
             nc.sync.dma_start(ds_tab[b:P:16, :].bitcast(I32), d_scales[0][b:16:2, :].bitcast(I32))
         gs_t = held([P, PACK], F32, "gs_t")
         nc.sync.dma_start(gs_t[:], gs.rearrange("(p t) o -> p (t o)", t=PACK))
         n1_t = load_list(n1, "n1_t")
         tab_v = tab.rearrange("(p t) j -> p t j", t=PACK)
-        tab_t = [held([P, J], F32, "tab%d" % t) for t in range(PACK)]
-        nc.sync.dma_start(tab_t[0][:], tab_v[:, 0, :])
+        nc.sync.dma_start(tab_t[0][:, :J], tab_v[:, 0, :])
         n2_t = load_list(n2, "n2_t")
         for t in range(1, PACK):
-            nc.sync.dma_start(tab_t[t][:], tab_v[:, t, :])
+            nc.sync.dma_start(tab_t[t][:, :J], tab_v[:, t, :])
         dw_tab = held([P, G], U32, "dw_tab")
         nc.sync.dma_start(dw_tab[:].bitcast(I32), d_words[0].rearrange("p n t -> p (n t)").bitcast(I32))
         n4_t = load_list(n4, "n4_t")
         n3_t = load_list(n3, "n3_t")
 
-        xs_g = held([P, S], U8, "xs_g")
-        nc.vector.tensor_copy(xs_g[:], xs_tab[:].indirect(offs_t[:]))
         ww = held([P, 2 * H], U8, "ww")
         nc.vector.tensor_copy(
             ww[:].rearrange("p (t m b) -> p t m b", t=PACK, b=2),
             ww_raw[:].rearrange("p (m t b) -> p t m b", t=PACK, b=2),
         )
+        xs_g = held([P, S], U8, "xs_g")
+        nc.vector.tensor_copy(xs_g[:], xs_tab[:].indirect(offs_t[:]))
         xw_g = held([P, S], U32, "xw_g")
         nc.vector.tensor_copy(xw_g[:], xw_tab[:].indirect(offs_t[:]))
         ws = held([P, H], U8, "ws")
@@ -100,11 +102,11 @@ def tile_picked_densekindgcube_none_po_kernel(
         gs_half = held([P, PACK], F32, "gs_half")
         nc.scalar.activation(gs_half[:], gs_t[:], ACT.Copy, scale=-0.5)
 
-        y_plain, y_win = [], []
+        y_ps = [psum.tile([P, S], F32, name="y_ps%d" % t, tag="bank%d" % t) for t in range(PACK)]
+        y_win = [held([P, 2 * S], F32, "y_win%d" % t) for t in range(PACK)]
         for t in range(PACK):
-            y_ps = psum.tile([P, S], F32, name="y_ps%d" % t)
             nc.tensor.matmul_mx(
-                y_ps[:],
+                y_ps[t][:],
                 lhsT=ww[:, 2 * P * t : 2 * P * (t + 1)].bitcast(FP4X4),
                 lhsT_scale=ws[:, P * t : P * (t + 1)],
                 rhs=xw_g[:].bitcast(FP8X4),
@@ -112,10 +114,13 @@ def tile_picked_densekindgcube_none_po_kernel(
                 start=True,
                 stop=True,
             )
-            y_plain.append(held([P, S], F32, "y_plain%d" % t))
-            y_win.append(held([P, S], F32, "y_win%d" % t))
-            nc.scalar.activation(y_plain[t][:], y_ps[:], ACT.Copy, scale=gs_t[:, t : t + 1])
-            nc.scalar.activation(y_win[t][:], y_ps[:], ACT.Copy, scale=gs_half[:, t : t + 1])
+        for t in range(PACK + 1):
+            if t < PACK:
+                nc.scalar.activation(y_win[t][:, S:], y_ps[t][:], ACT.Copy, scale=gs_t[:, t : t + 1])
+            if t > 0:
+                nc.scalar.activation(
+                    y_win[t - 1][:, :S], y_ps[t - 1][:], ACT.Copy, scale=gs_half[:, t - 1 : t]
+                )
 
         ds_g = held([P, H], U8, "ds_g")
         nc.vector.tensor_copy(ds_g[:], ds_tab[:].indirect(k1_t[:]))
@@ -127,139 +132,126 @@ def tile_picked_densekindgcube_none_po_kernel(
             src = c % 2 + 16 * (c // 2)
             nc.sync.dma_start(ds_mm[c:P:32, :].bitcast(I32), ds_d[src:P:32, :].bitcast(I32))
 
-        dw_g = held([P, H], U32, "dw_g")
-        dw = held([P, H], U32, "dw")
         z_codes = held([P, S], U32, "z_codes")
         z_scales = held([P, S], U8, "z_scales")
-        h_ps = [psum.tile([P, S], F32, name="h_ps%d" % t) for t in range(PACK)]
+        h_ps = {}
+        h_plain = held([P, PACK, HALF], F32, "h_plain")
         h_win = [held([P, S], F32, "h_win%d" % t) for t in range(PACK)]
+        dw = held([P, H], U32, "dw")
 
-        h_plain = [held([P, S - Z_SLICES[-1][1]], F32, "h_plain%d" % t) for t in range(PACK)]
+        def interleave(copy, dst, src):
+            copy(dst.rearrange("p (c t) -> p c t", t=PACK), src.rearrange("p t c -> p c t"))
 
-        def interleave(copy, src, n, name):
-            dst = held([P, n * PACK], BF16, name)
-            copy(dst[:].rearrange("p (c t) -> p c t", t=PACK), src[:].rearrange("p t c -> p c t"))
+        def round_half(src, i, name):
+            dst = held([P, HALF * PACK], BF16, name)
+            if i == 0:
+                interleave(nc.scalar.copy, dst[:], src)
+            else:
+                cut = SCALAR_SHARE
+                interleave(nc.scalar.copy, dst[:, : cut * PACK], src[:, :, :cut])
+                interleave(nc.vector.tensor_copy, dst[:, cut * PACK :], src[:, :, cut:])
             return dst
 
-        def quantize(codes, scales, src, c0, n):
-            nc.vector.quantize_mx(codes[:, c0 : c0 + n].bitcast(FP8X4), scales[:, c0 : c0 + n], src[:])
+        def quantize(codes, scales, src, i):
+            c = slice(i * HALF, (i + 1) * HALF)
+            nc.vector.quantize_mx(codes[:, c].bitcast(FP8X4), scales[:, c], src[:])
 
-        def second_product(c0, n, last):
-            for t in range(PACK):
+        def second_product(i):
+            c = slice(i * HALF, (i + 1) * HALF)
+            for t in (0, 2, 1, 3):
+                h_ps[i, t] = psum.tile([P, HALF], F32, name="h_ps%d%d" % (i, t), tag="bank%d" % (PACK * (1 - i) + t))
+                acc = h_ps[i, t][:]
                 nc.tensor.matmul_mx(
-                    h_ps[t][:, c0 : c0 + n],
+                    acc,
                     lhsT=dw[:, P * t : P * (t + 1)].bitcast(FP8X4),
                     lhsT_scale=ds_mm[:, P * t : P * (t + 1)],
-                    rhs=z_codes[:, c0 : c0 + n].bitcast(FP8X4),
-                    rhs_scale=z_scales[:, c0 : c0 + n],
+                    rhs=z_codes[:, c].bitcast(FP8X4),
+                    rhs_scale=z_scales[:, c],
                     start=True,
                     stop=True,
                 )
-                if last and t < 2:
-                    nc.vector.tensor_scalar(
-                        h_win[t][:, c0 : c0 + n], h_ps[t][:, c0 : c0 + n], 1.0 / 128, None, ALU.mult
-                    )
+                if i == 1 and t == 2:
+                    nc.vector.tensor_scalar(h_win[t][:, c], acc, 1.0 / 128, None, ALU.mult)
                 else:
-                    nc.scalar.activation(
-                        h_win[t][:, c0 : c0 + n], h_ps[t][:, c0 : c0 + n], ACT.Copy, scale=1.0 / 128
-                    )
-                if not last:
-                    nc.scalar.copy(h_plain[t][:, c0 : c0 + n], h_ps[t][:, c0 : c0 + n])
-
-        steps = [(i, t) for i in range(len(Z_SLICES)) for t in range(PACK)]
-        z = {}
-        z_bf = {}
-        prod = {}
-
-        def kind_term(i, t):
-            c0, n = Z_SLICES[i]
-            a = ring.tile([P, n], F32, name="a", align_bytes=64)
-            nc.vector.tensor_tensor(
-                a[:], tab_t[t][:].indirect(cols(n1_t, c0, n)), y_plain[t][:, c0 : c0 + n], ALU.mult
-            )
-            prod[i, t] = a
-
-        kind_term(*steps[0])
-        for k, (i, t) in enumerate(steps):
-            c0, n = Z_SLICES[i]
-            if k + 1 < len(steps):
-                kind_term(*steps[k + 1])
-            if t == 0:
-                z[i] = held([P, PACK, n], F32, "z%d" % i, tag="z_bf0" if i == 2 else None)
-            nc.vector.tensor_tensor(
-                z[i][:, t, :], y_win[t][:].indirect(cols(n2_t, c0, n)), prod[i, t][:], ALU.add
-            )
-            last = i == len(Z_SLICES) - 1
-            if t == PACK - 1:
-                copy = nc.vector.tensor_copy if last else nc.scalar.copy
-                z_bf[i] = interleave(copy, z[i], n, "z_bf%d" % i)
+                    nc.scalar.activation(h_win[t][:, c], acc, ACT.Copy, scale=1.0 / 128)
                 if i == 0:
-                    nc.vector.tensor_copy(dw_g[:], dw_tab[:].indirect(k1_t[:]))
-                    nc.vector.tensor_copy(
-                        dw[:].rearrange("p (t m) -> p t m", t=PACK),
-                        dw_g[:].rearrange("p (m t) -> p t m", t=PACK),
-                    )
-                if last:
-                    quantize(z_codes, z_scales, z_bf[i], c0, n)
-                    second_product(c0, n, True)
-            if t == 2 and i > 0:
-                quantize(z_codes, z_scales, z_bf[i - 1], *Z_SLICES[i - 1])
-                second_product(*Z_SLICES[i - 1], False)
+                    nc.scalar.copy(h_plain[:, t, :], acc)
+
+        z = held([P, PACK, S], F32, "z")
+
+        def kind_term(t, c0, n, tag):
+            a = held([P, n], F32, "a%d_%d" % (t, c0), tag)
+            nc.vector.tensor_tensor(
+                a[:], tab_t[t][:].indirect(cols(n1_t, c0, n)), y_win[t][:, S + c0 : S + c0 + n], ALU.mult
+            )
+            return a
+
+        def add_place_term(t, c0, n, a):
+            nc.vector.tensor_tensor(
+                z[:, t, c0 : c0 + n], y_win[t][:].indirect(cols(n2_t, c0, n)), a, ALU.add
+            )
+
+        a0 = kind_term(0, 0, S, None)
+        a1 = kind_term(1, 0, S, None)
+        add_place_term(0, 0, S, a0[:])
+        a2 = kind_term(2, 0, S, None)
+        add_place_term(1, 0, S, a1[:])
+        a3 = kind_term(3, 0, HALF, "dw_g")
+        add_place_term(2, 0, HALF, a2[:, :HALF])
+        add_place_term(3, 0, HALF, a3[:])
+        z_bf = round_half(z[:, :, :HALF], 0, "z_bf0")
+        dw_g = held([P, H], U32, "dw_g")
+        nc.vector.tensor_copy(dw_g[:], dw_tab[:].indirect(k1_t[:]))
+        add_place_term(2, HALF, HALF, a2[:, HALF:])
+        nc.vector.tensor_copy(
+            dw[:].rearrange("p (t m) -> p t m", t=PACK), dw_g[:].rearrange("p (m t) -> p t m", t=PACK)
+        )
+        quantize(z_codes, z_scales, z_bf, 0)
+        second_product(0)
+        a3 = kind_term(3, HALF, HALF, "z_bf0")
+        add_place_term(3, HALF, HALF, a3[:])
+        z_bf = round_half(z[:, :, HALF:], 1, "z_bf1")
+        quantize(z_codes, z_scales, z_bf, 1)
+        second_product(1)
 
         out_v = out_0.rearrange("(p t) j -> p t j", t=PACK)
         words_v = out_1[0].rearrange("p n t -> p (n t)").bitcast(I32)
         o_codes = held([P, S], U32, "o_codes")
         o_scales = held([P, S], U8, "o_scales")
-        steps = [(i, t) for i in range(len(OUT_SLICES)) for t in range(PACK)]
-        o = [held([P, PACK, n], F32, "o%d" % i) for i, (c0, n) in enumerate(OUT_SLICES)]
-        o_bf = {}
-        gate = {}
-
-        def first_step(i, t):
-            c0, n = OUT_SLICES[i]
-            s = ring.tile([P, n], F32, name="s", align_bytes=64)
-            nc.scalar.activation(s[:], h_win[t][:].indirect(cols(n4_t, c0, n)), ACT.Sigmoid, scale=16.0)
-            u = ring.tile([P, n], F32, name="u", align_bytes=64)
-            if i == len(OUT_SLICES) - 1:
-                nc.vector.scalar_tensor_tensor(
-                    u[:], s[:], half[:], h_ps[t][:, c0 : c0 + n], ALU.subtract, ALU.mult
+        s = [held([P, PACK, HALF], F32, "s%d" % i) for i in range(2)]
+        u = [held([P, PACK, HALF], F32, "u%d" % i) for i in range(2)]
+        o = [held([P, PACK, HALF], F32, "o%d" % i) for i in range(2)]
+        for i in range(2):
+            for t in range(PACK):
+                nc.scalar.activation(
+                    s[i][:, t, :], h_win[t][:].indirect(cols(n4_t, i * HALF, HALF)), ACT.Sigmoid, scale=16.0
                 )
-            else:
-                nc.vector.tensor_tensor(
-                    u[:], h_win[t][:].indirect(cols(n3_t, c0, n)), h_plain[t][:, c0 : c0 + n], ALU.mult
-                )
-            gate[i, t] = (s, u)
 
-        def second_step(i, t):
-            c0, n = OUT_SLICES[i]
-            s, u = gate[i, t]
-            if i == len(OUT_SLICES) - 1:
-                nc.vector.tensor_tensor(
-                    o[i][:, t, :], h_win[t][:].indirect(cols(n3_t, c0, n)), u[:], ALU.mult
-                )
-            else:
-                nc.vector.scalar_tensor_tensor(o[i][:, t, :], s[:], half[:], u[:], ALU.subtract, ALU.mult)
+        def tanh_times(out, sig, other):
+            nc.vector.scalar_tensor_tensor(out, sig, half[:], other, ALU.subtract, ALU.mult)
 
-        def planes(i):
-            c0, n = OUT_SLICES[i]
-            quantize(o_codes, o_scales, o_bf[i], c0, n)
-            nc.sync.dma_start(words_v[:, c0 : c0 + n], o_codes[:, c0 : c0 + n].bitcast(I32))
+        def place_times(out, i, t, other):
+            nc.vector.tensor_tensor(out, h_win[t][:].indirect(cols(n3_t, i * HALF, HALF)), other, ALU.mult)
 
-        first_step(*steps[0])
-        for k, (i, t) in enumerate(steps):
-            c0, n = OUT_SLICES[i]
-            if k + 1 < len(steps):
-                first_step(*steps[k + 1])
-            second_step(i, t)
-            last = i == len(OUT_SLICES) - 1
-            if t == PACK - 1:
-                nc.sync.dma_start(out_v[:, :, c0 : c0 + n], o[i][:])
-                copy = nc.vector.tensor_copy if last else nc.scalar.copy
-                o_bf[i] = interleave(copy, o[i], n, "o_bf%d" % i)
-                if last:
-                    planes(i)
-            if t == 2 and i > 0:
-                planes(i - 1)
+        def planes(i, src):
+            quantize(o_codes, o_scales, src, i)
+            c = slice(i * HALF, (i + 1) * HALF)
+            nc.sync.dma_start(words_v[:, c], o_codes[:, c].bitcast(I32))
+
+        for t in (0, 2, 1, 3):
+            place_times(u[0][:, t, :], 0, t, h_plain[:, t, :])
+        tanh_times(o[0][:], s[0][:], u[0][:])
+        nc.sync.dma_start(out_v[:, :, :HALF], o[0][:])
+        o_bf0 = round_half(o[0][:], 0, "o_bf0")
+        for t in range(PACK + 1):
+            if t < PACK:
+                tanh_times(u[1][:, t, :], s[1][:, t, :], h_ps[1, t][:])
+            if t > 0:
+                place_times(o[1][:, t - 1, :], 1, t - 1, u[1][:, t - 1, :])
+            if t in (2, 4):
+                nc.sync.dma_start(out_v[:, t - 2 : t, HALF:], o[1][:, t - 2 : t, :])
+        planes(0, o_bf0)
+        planes(1, round_half(o[1][:], 1, "o_bf1"))
         for r in range(4):
             queue = nc.scalar if r % 2 else nc.sync
             queue.dma_start(out_2[0][r:16:4, :].bitcast(I32), o_scales[r:P:32, :].bitcast(I32))

@@ -19,7 +19,7 @@ K, T, S, H, J, G = 512, 2048, 512, 512, 512, 2048
 FLOPS = 2 * K * H * S + 2 * K * H * S
 
 HALF = S // 2
-SCALAR_SHARE = 96
+QUARTER = S // 4
 
 
 def tile_picked_densekindgcube_none_po_kernel(
@@ -140,79 +140,79 @@ def tile_picked_densekindgcube_none_po_kernel(
         dw = held([P, H], U32, "dw")
 
         def interleave(copy, dst, src):
-            copy(dst.rearrange("p (c t) -> p c t", t=PACK), src.rearrange("p t c -> p c t"))
-
-        def round_half(src, i, name):
-            dst = held([P, HALF * PACK], BF16, name)
-            if i == 0:
-                interleave(nc.scalar.copy, dst[:], src)
-            else:
-                cut = SCALAR_SHARE
-                interleave(nc.scalar.copy, dst[:, : cut * PACK], src[:, :, :cut])
-                interleave(nc.vector.tensor_copy, dst[:, cut * PACK :], src[:, :, cut:])
-            return dst
+            copy(
+                dst.rearrange("p (c i t) -> p c t i", i=4, t=PACK), src.rearrange("p t (c i) -> p c t i", i=4)
+            )
 
         def quantize(codes, scales, src, i):
             c = slice(i * HALF, (i + 1) * HALF)
             nc.vector.quantize_mx(codes[:, c].bitcast(FP8X4), scales[:, c], src[:])
 
-        def second_product(i):
+        def second_product(acc, i, t):
             c = slice(i * HALF, (i + 1) * HALF)
-            for t in (0, 2, 1, 3):
-                h_ps[i, t] = psum.tile([P, HALF], F32, name="h_ps%d%d" % (i, t), tag="bank%d" % (PACK * (1 - i) + t))
-                acc = h_ps[i, t][:]
-                nc.tensor.matmul_mx(
-                    acc,
-                    lhsT=dw[:, P * t : P * (t + 1)].bitcast(FP8X4),
-                    lhsT_scale=ds_mm[:, P * t : P * (t + 1)],
-                    rhs=z_codes[:, c].bitcast(FP8X4),
-                    rhs_scale=z_scales[:, c],
-                    start=True,
-                    stop=True,
-                )
-                if i == 1 and t == 2:
-                    nc.vector.tensor_scalar(h_win[t][:, c], acc, 1.0 / 128, None, ALU.mult)
-                else:
-                    nc.scalar.activation(h_win[t][:, c], acc, ACT.Copy, scale=1.0 / 128)
-                if i == 0:
-                    nc.scalar.copy(h_plain[:, t, :], acc)
+            nc.tensor.matmul_mx(
+                acc,
+                lhsT=dw[:, P * t : P * (t + 1)].bitcast(FP8X4),
+                lhsT_scale=ds_mm[:, P * t : P * (t + 1)],
+                rhs=z_codes[:, c].bitcast(FP8X4),
+                rhs_scale=z_scales[:, c],
+                start=True,
+                stop=True,
+            )
 
         z = held([P, PACK, S], F32, "z")
 
-        def kind_term(t, c0, n, tag):
-            a = held([P, n], F32, "a%d_%d" % (t, c0), tag)
+        def kind_term(a, t, c0, n):
             nc.vector.tensor_tensor(
-                a[:], tab_t[t][:].indirect(cols(n1_t, c0, n)), y_win[t][:, S + c0 : S + c0 + n], ALU.mult
+                a, tab_t[t][:].indirect(cols(n1_t, c0, n)), y_win[t][:, S + c0 : S + c0 + n], ALU.mult
             )
-            return a
 
         def add_place_term(t, c0, n, a):
             nc.vector.tensor_tensor(
                 z[:, t, c0 : c0 + n], y_win[t][:].indirect(cols(n2_t, c0, n)), a, ALU.add
             )
 
-        a0 = kind_term(0, 0, S, None)
-        a1 = kind_term(1, 0, S, None)
-        add_place_term(0, 0, S, a0[:])
-        a2 = kind_term(2, 0, S, None)
-        add_place_term(1, 0, S, a1[:])
-        a3 = kind_term(3, 0, HALF, "dw_g")
-        add_place_term(2, 0, HALF, a2[:, :HALF])
-        add_place_term(3, 0, HALF, a3[:])
-        z_bf = round_half(z[:, :, :HALF], 0, "z_bf0")
+        a_whole = held([P, 2, S], F32, "a_whole")
+        a_first = held([P, 2, HALF], F32, "a_first", "dw_g")
+        kind_term(a_whole[:, 0, :], 0, 0, S)
+        kind_term(a_whole[:, 1, :], 1, 0, S)
+        add_place_term(0, 0, S, a_whole[:, 0, :])
+        kind_term(a_first[:, 0, :], 2, 0, HALF)
+        add_place_term(1, 0, S, a_whole[:, 1, :])
+        kind_term(a_first[:, 1, :], 3, 0, HALF)
+        add_place_term(2, 0, HALF, a_first[:, 0, :])
+        add_place_term(3, 0, HALF, a_first[:, 1, :])
+        z_bf0 = held([P, HALF * PACK], BF16, "z_bf0")
+        interleave(nc.scalar.copy, z_bf0[:], z[:, :, :HALF])
         dw_g = held([P, H], U32, "dw_g")
         nc.vector.tensor_copy(dw_g[:], dw_tab[:].indirect(k1_t[:]))
-        add_place_term(2, HALF, HALF, a2[:, HALF:])
         nc.vector.tensor_copy(
-            dw[:].rearrange("p (t m) -> p t m", t=PACK), dw_g[:].rearrange("p (m t) -> p t m", t=PACK)
+            dw[:].rearrange("p (t c i) -> p c t i", t=PACK, i=4),
+            dw_g[:].rearrange("p (c i t) -> p c t i", t=PACK, i=4),
         )
-        quantize(z_codes, z_scales, z_bf, 0)
-        second_product(0)
-        a3 = kind_term(3, HALF, HALF, "z_bf0")
-        add_place_term(3, HALF, HALF, a3[:])
-        z_bf = round_half(z[:, :, HALF:], 1, "z_bf1")
-        quantize(z_codes, z_scales, z_bf, 1)
-        second_product(1)
+        quantize(z_codes, z_scales, z_bf0, 0)
+        for u2 in range(2):
+            pair = psum.tile([P, 2, HALF], F32, name="h_pair%d" % u2, tag="bank%d" % (PACK + u2))
+            for e in range(2):
+                second_product(pair[:, e, :], 0, 2 * u2 + e)
+            for e in range(2):
+                nc.scalar.activation(h_win[2 * u2 + e][:, :HALF], pair[:, e, :], ACT.Copy, scale=1.0 / 128)
+            nc.scalar.copy(h_plain[:, 2 * u2 : 2 * u2 + 2, :], pair[:])
+        a_second = held([P, 2, HALF], F32, "a_second", "z_bf0")
+        for e in range(2):
+            kind_term(a_second[:, e, :], 2 + e, HALF, HALF)
+        for e in range(2):
+            add_place_term(2 + e, HALF, HALF, a_second[:, e, :])
+        z_bf1 = held([P, HALF * PACK], BF16, "z_bf1")
+        interleave(nc.vector.tensor_copy, z_bf1[:], z[:, :, HALF:])
+        quantize(z_codes, z_scales, z_bf1, 1)
+        for t in (0, 2, 1, 3):
+            h_ps[t] = psum.tile([P, HALF], F32, name="h_ps%d" % t, tag="bank%d" % t)
+            second_product(h_ps[t][:], 1, t)
+            if t == 2:
+                nc.vector.tensor_scalar(h_win[t][:, HALF:], h_ps[t][:], 1.0 / 128, None, ALU.mult)
+            else:
+                nc.scalar.activation(h_win[t][:, HALF:], h_ps[t][:], ACT.Copy, scale=1.0 / 128)
 
         out_v = out_0.rearrange("(p t) j -> p t j", t=PACK)
         words_v = out_1[0].rearrange("p n t -> p (n t)").bitcast(I32)
@@ -230,8 +230,8 @@ def tile_picked_densekindgcube_none_po_kernel(
         def tanh_times(out, sig, other):
             nc.vector.scalar_tensor_tensor(out, sig, half[:], other, ALU.subtract, ALU.mult)
 
-        def place_times(out, i, t, other):
-            nc.vector.tensor_tensor(out, h_win[t][:].indirect(cols(n3_t, i * HALF, HALF)), other, ALU.mult)
+        def place_times(out, t, c0, n, other):
+            nc.vector.tensor_tensor(out, h_win[t][:].indirect(cols(n3_t, c0, n)), other, ALU.mult)
 
         def planes(i, src):
             quantize(o_codes, o_scales, src, i)
@@ -239,19 +239,24 @@ def tile_picked_densekindgcube_none_po_kernel(
             nc.sync.dma_start(words_v[:, c], o_codes[:, c].bitcast(I32))
 
         for t in (0, 2, 1, 3):
-            place_times(u[0][:, t, :], 0, t, h_plain[:, t, :])
+            place_times(u[0][:, t, :], t, 0, HALF, h_plain[:, t, :])
         tanh_times(o[0][:], s[0][:], u[0][:])
         nc.sync.dma_start(out_v[:, :, :HALF], o[0][:])
-        o_bf0 = round_half(o[0][:], 0, "o_bf0")
-        for t in range(PACK + 1):
-            if t < PACK:
-                tanh_times(u[1][:, t, :], s[1][:, t, :], h_ps[1, t][:])
-            if t > 0:
-                place_times(o[1][:, t - 1, :], 1, t - 1, u[1][:, t - 1, :])
-            if t in (2, 4):
-                nc.sync.dma_start(out_v[:, t - 2 : t, HALF:], o[1][:, t - 2 : t, :])
+        o_bf0 = held([P, HALF * PACK], BF16, "o_bf0")
+        interleave(nc.scalar.copy, o_bf0[:], o[0][:])
+        o_bf1 = held([P, HALF * PACK], BF16, "o_bf1")
+        tanh_times(u[1][:, 0, :], s[1][:, 0, :], h_ps[0][:])
+        for t in range(PACK - 1):
+            tanh_times(u[1][:, t + 1, :], s[1][:, t + 1, :], h_ps[t + 1][:])
+            place_times(o[1][:, t, :], t, HALF, HALF, u[1][:, t, :])
+        nc.sync.dma_start(out_v[:, :3, HALF:], o[1][:, :3, :])
+        place_times(o[1][:, 3, :QUARTER], 3, HALF, QUARTER, u[1][:, 3, :QUARTER])
+        interleave(nc.scalar.copy, o_bf1[:, : QUARTER * PACK], o[1][:, :, :QUARTER])
+        place_times(o[1][:, 3, QUARTER:], 3, HALF + QUARTER, QUARTER, u[1][:, 3, QUARTER:])
+        nc.sync.dma_start(out_v[:, 3, HALF:], o[1][:, 3, :])
         planes(0, o_bf0)
-        planes(1, round_half(o[1][:], 1, "o_bf1"))
+        interleave(nc.vector.tensor_copy, o_bf1[:, QUARTER * PACK :], o[1][:, :, QUARTER:])
+        planes(1, o_bf1)
         for r in range(4):
             queue = nc.scalar if r % 2 else nc.sync
             queue.dma_start(out_2[0][r:16:4, :].bitcast(I32), o_scales[r:P:32, :].bitcast(I32))

@@ -55,8 +55,7 @@ def tile_picked_densekindgcube_none_po_kernel(
         tab_t = [held([P, 2 * J], F32, "tab%d" % t) for t in range(PACK)]
         nc.gpsimd.memset(zero[:], 0.0)
         for t in range(PACK):
-            engine = nc.gpsimd if t % 2 else nc.vector
-            engine.memset(tab_t[t][:, J:], 0.0)
+            nc.vector.memset(tab_t[t][:, J:], 0.0)
         nc.vector.memset(ds_mm[:].bitcast(I32), 0)
 
         ww_raw = held([P, 2 * H], U8, "ww_raw")
@@ -71,10 +70,9 @@ def tile_picked_densekindgcube_none_po_kernel(
         for r in range(4):
             nc.sync.dma_start(ws_raw[r:P:32, :].bitcast(I32), w1_scales[0][r:16:4, :].bitcast(I32))
         nc.scalar.activation(half[:], zero[:], ACT.Sigmoid)
-        for b in range(2):
-            nc.sync.dma_start(ds_tab[b:P:16, :].bitcast(I32), d_scales[0][b:16:2, :].bitcast(I32))
+        nc.sync.dma_start(ds_tab[0:P:8, :].bitcast(I32), d_scales[0].bitcast(I32))
         gs_t = held([P, PACK], F32, "gs_t")
-        nc.sync.dma_start(gs_t[:], gs.rearrange("(p t) o -> p (t o)", t=PACK))
+        nc.gpsimd.dma_start(gs_t[:], gs.rearrange("(p t) o -> p (t o)", t=PACK))
         n1_t = load_list(n1, "n1_t")
         tab_v = tab.rearrange("(p t) j -> p t j", t=PACK)
         nc.sync.dma_start(tab_t[0][:, :J], tab_v[:, 0, :])
@@ -129,7 +127,7 @@ def tile_picked_densekindgcube_none_po_kernel(
             ds_d[:].rearrange("p (t m) -> p t m", t=PACK), ds_g[:].rearrange("p (m t) -> p t m", t=PACK)
         )
         for c in range(4):
-            src = c % 2 + 16 * (c // 2)
+            src = 8 * c
             nc.sync.dma_start(ds_mm[c:P:32, :].bitcast(I32), ds_d[src:P:32, :].bitcast(I32))
 
         z_codes = held([P, S], U32, "z_codes")
@@ -249,7 +247,7 @@ def tile_picked_densekindgcube_none_po_kernel(
         for t in range(PACK - 1):
             tanh_times(u[1][:, t + 1, :], s[1][:, t + 1, :], h_ps[t + 1][:])
             place_times(o[1][:, t, :], t, HALF, HALF, u[1][:, t, :])
-        nc.sync.dma_start(out_v[:, :3, HALF:], o[1][:, :3, :])
+            nc.sync.dma_start(out_v[:, t, HALF:], o[1][:, t, :])
         place_times(o[1][:, 3, :QUARTER], 3, HALF, QUARTER, u[1][:, 3, :QUARTER])
         interleave(nc.scalar.copy, o_bf1[:, : QUARTER * PACK], o[1][:, :, :QUARTER])
         place_times(o[1][:, 3, QUARTER:], 3, HALF + QUARTER, QUARTER, u[1][:, 3, QUARTER:])

from contextlib import ExitStack

import concourse.mybir as mybir

F32 = mybir.dt.float32
BF16 = mybir.dt.bfloat16
I32 = mybir.dt.int32
U32 = mybir.dt.uint32
U16 = mybir.dt.uint16
U8 = mybir.dt.uint8
FP8X4 = mybir.dt.float8_e4m3fn_x4
FP4X4 = mybir.dt.float4_e2m1fn_x4
ALU = mybir.AluOpType
ACT = mybir.ActivationFunctionType

P = 128
PACK = 4
K, T, S, H, J, G = 512, 2048, 512, 512, 512, 2048
FLOPS = 2 * K * H * S + 2 * K * H * S

HALF = S // 2
QUARTER = S // 4


def tile_picked_densekindgcube_none_po_kernel(
    tc, x_words, x_scales, w1_words, w1_scales, tab, gs, d_words, d_scales,
    offs, n1, n2, k1, n3, n4, out_0, out_1, out_2,
):
    nc = tc.nc
    with ExitStack() as ctx:
        keep = ctx.enter_context(tc.tile_pool(name="keep", bufs=1))
        psum = ctx.enter_context(tc.psum_pool(name="psum", bufs=1))

        def held(shape, dtype, name, tag=None):
            return keep.tile(shape, dtype, name=name, tag=tag or name, align_bytes=64)

        def load_list(src, name):
            t = held([P, S // 16], U16, name)
            nc.sync.dma_start(t[:], src)
            return t

        def cols(lst, c0, n):
            return lst[:, c0 // 16 : (c0 + n) // 16]

        xs_tab = held([P, T], U8, "xs_tab")
        ws_raw = held([P, H], U8, "ws_raw")
        ds_tab = held([P, G], U8, "ds_tab")
        ds_mm = held([P, H], U8, "ds_mm")
        zero = held([P, 1], F32, "zero")
        half = held([P, 1], F32, "half")
        nc.gpsimd.memset(xs_tab[:, : T // 2].bitcast(I32), 0)
        nc.vector.memset(xs_tab[:, T // 2 :].bitcast(I32), 0)
        nc.vector.memset(ws_raw[:].bitcast(I32), 0)
        nc.vector.memset(ds_tab[:].bitcast(I32), 0)
        tab_t = [held([P, 2 * J], F32, "tab%d" % t) for t in range(PACK)]
        nc.gpsimd.memset(zero[:], 0.0)
        for t in range(PACK):
            nc.vector.memset(tab_t[t][:, J:], 0.0)
        nc.vector.memset(ds_mm[:].bitcast(I32), 0)

        ww_raw = held([P, 2 * H], U8, "ww_raw")
        nc.scalar.dma_start(ww_raw[:].bitcast(I32), w1_words[0].bitcast(I32))
        offs_t = load_list(offs, "offs_t")
        k1_t = load_list(k1, "k1_t")
        for r in range(4):
            queue = nc.scalar if r % 2 else nc.sync
            queue.dma_start(xs_tab[r:P:32, :].bitcast(I32), x_scales[0][r:16:4, :].bitcast(I32))
        xw_tab = held([P, T], U32, "xw_tab")
        nc.sync.dma_start(xw_tab[:].bitcast(I32), x_words[0].rearrange("p n t -> p (n t)").bitcast(I32))
        for r in range(4):
            nc.sync.dma_start(ws_raw[r:P:32, :].bitcast(I32), w1_scales[0][r:16:4, :].bitcast(I32))
        nc.scalar.activation(half[:], zero[:], ACT.Sigmoid)
        nc.sync.dma_start(ds_tab[0:P:8, :].bitcast(I32), d_scales[0].bitcast(I32))
        gs_t = held([P, PACK], F32, "gs_t")
        nc.gpsimd.dma_start(gs_t[:], gs.rearrange("(p t) o -> p (t o)", t=PACK))
        n1_t = load_list(n1, "n1_t")
        tab_v = tab.rearrange("(p t) j -> p t j", t=PACK)
        nc.sync.dma_start(tab_t[0][:, :J], tab_v[:, 0, :])
        n2_t = load_list(n2, "n2_t")
        for t in range(1, PACK):
            nc.sync.dma_start(tab_t[t][:, :J], tab_v[:, t, :])
        dw_tab = held([P, G], U32, "dw_tab")
        nc.sync.dma_start(dw_tab[:].bitcast(I32), d_words[0].rearrange("p n t -> p (n t)").bitcast(I32))
        n4_t = load_list(n4, "n4_t")
        n3_t = load_list(n3, "n3_t")

        ww = held([P, 2 * H], U8, "ww")
        nc.vector.tensor_copy(
            ww[:].rearrange("p (t m b) -> p t m b", t=PACK, b=2),
            ww_raw[:].rearrange("p (m t b) -> p t m b", t=PACK, b=2),
        )
        xs_g = held([P, S], U8, "xs_g")
        nc.vector.tensor_copy(xs_g[:], xs_tab[:].indirect(offs_t[:]))
        xw_g = held([P, S], U32, "xw_g")
        nc.vector.tensor_copy(xw_g[:], xw_tab[:].indirect(offs_t[:]))
        ws = held([P, H], U8, "ws")
        nc.vector.tensor_copy(
            ws[:].rearrange("p (t m) -> p t m", t=PACK), ws_raw[:].rearrange("p (m t) -> p t m", t=PACK)
        )
        gs_half = held([P, PACK], F32, "gs_half")
        nc.scalar.activation(gs_half[:], gs_t[:], ACT.Copy, scale=-0.5)

        y_ps = [psum.tile([P, S], F32, name="y_ps%d" % t, tag="bank%d" % t) for t in range(PACK)]
        y_win = [held([P, 2 * S], F32, "y_win%d" % t) for t in range(PACK)]
        for t in range(PACK):
            nc.tensor.matmul_mx(
                y_ps[t][:],
                lhsT=ww[:, 2 * P * t : 2 * P * (t + 1)].bitcast(FP4X4),
                lhsT_scale=ws[:, P * t : P * (t + 1)],
                rhs=xw_g[:].bitcast(FP8X4),
                rhs_scale=xs_g[:],
                start=True,
                stop=True,
            )
        for t in range(PACK + 1):
            if t < PACK:
                nc.scalar.activation(y_win[t][:, S:], y_ps[t][:], ACT.Copy, scale=gs_t[:, t : t + 1])
            if t > 0:
                nc.scalar.activation(
                    y_win[t - 1][:, :S], y_ps[t - 1][:], ACT.Copy, scale=gs_half[:, t - 1 : t]
                )

        ds_g = held([P, H], U8, "ds_g")
        nc.vector.tensor_copy(ds_g[:], ds_tab[:].indirect(k1_t[:]))
        ds_d = held([P, H], U8, "ds_d")
        nc.vector.tensor_copy(
            ds_d[:].rearrange("p (t m) -> p t m", t=PACK), ds_g[:].rearrange("p (m t) -> p t m", t=PACK)
        )
        for c in range(4):
            src = 8 * c
            nc.sync.dma_start(ds_mm[c:P:32, :].bitcast(I32), ds_d[src:P:32, :].bitcast(I32))

        z_codes = held([P, S], U32, "z_codes")
        z_scales = held([P, S], U8, "z_scales")
        h_ps = {}
        h_plain = held([P, PACK, HALF], F32, "h_plain")
        h_win = [held([P, S], F32, "h_win%d" % t) for t in range(PACK)]
        dw = held([P, H], U32, "dw")

        def interleave(copy, dst, src):
            copy(
                dst.rearrange("p (c i t) -> p c t i", i=4, t=PACK), src.rearrange("p t (c i) -> p c t i", i=4)
            )

        def quantize(codes, scales, src, i):
            c = slice(i * HALF, (i + 1) * HALF)
            nc.vector.quantize_mx(codes[:, c].bitcast(FP8X4), scales[:, c], src[:])

        def second_product(acc, i, t):
            c = slice(i * HALF, (i + 1) * HALF)
            nc.tensor.matmul_mx(
                acc,
                lhsT=dw[:, P * t : P * (t + 1)].bitcast(FP8X4),
                lhsT_scale=ds_mm[:, P * t : P * (t + 1)],
                rhs=z_codes[:, c].bitcast(FP8X4),
                rhs_scale=z_scales[:, c],
                start=True,
                stop=True,
            )

        z = held([P, PACK, S], F32, "z")

        def kind_term(a, t, c0, n):
            nc.vector.tensor_tensor(
                a, tab_t[t][:].indirect(cols(n1_t, c0, n)), y_win[t][:, S + c0 : S + c0 + n], ALU.mult
            )

        def add_place_term(t, c0, n, a):
            nc.vector.tensor_tensor(
                z[:, t, c0 : c0 + n], y_win[t][:].indirect(cols(n2_t, c0, n)), a, ALU.add
            )

        a_whole = held([P, 2, S], F32, "a_whole")
        a_first = held([P, 2, HALF], F32, "a_first", "dw_g")
        kind_term(a_whole[:, 0, :], 0, 0, S)
        kind_term(a_whole[:, 1, :], 1, 0, S)
        add_place_term(0, 0, S, a_whole[:, 0, :])
        kind_term(a_first[:, 0, :], 2, 0, HALF)
        add_place_term(1, 0, S, a_whole[:, 1, :])
        kind_term(a_first[:, 1, :], 3, 0, HALF)
        add_place_term(2, 0, HALF, a_first[:, 0, :])
        add_place_term(3, 0, HALF, a_first[:, 1, :])
        z_bf0 = held([P, HALF * PACK], BF16, "z_bf0")
        interleave(nc.scalar.copy, z_bf0[:], z[:, :, :HALF])
        dw_g = held([P, H], U32, "dw_g")
        nc.vector.tensor_copy(dw_g[:], dw_tab[:].indirect(k1_t[:]))
        nc.vector.tensor_copy(
            dw[:].rearrange("p (t c i) -> p c t i", t=PACK, i=4),
            dw_g[:].rearrange("p (c i t) -> p c t i", t=PACK, i=4),
        )
        quantize(z_codes, z_scales, z_bf0, 0)
        for u2 in range(2):
            pair = psum.tile([P, 2, HALF], F32, name="h_pair%d" % u2, tag="bank%d" % (PACK + u2))
            for e in range(2):
                second_product(pair[:, e, :], 0, 2 * u2 + e)
            for e in range(2):
                nc.scalar.activation(h_win[2 * u2 + e][:, :HALF], pair[:, e, :], ACT.Copy, scale=1.0 / 128)
            nc.scalar.copy(h_plain[:, 2 * u2 : 2 * u2 + 2, :], pair[:])
        a_second = held([P, 2, HALF], F32, "a_second", "z_bf0")
        for e in range(2):
            kind_term(a_second[:, e, :], 2 + e, HALF, HALF)
        for e in range(2):
            add_place_term(2 + e, HALF, HALF, a_second[:, e, :])
        z_bf1 = held([P, HALF * PACK], BF16, "z_bf1")
        interleave(nc.vector.tensor_copy, z_bf1[:], z[:, :, HALF:])
        quantize(z_codes, z_scales, z_bf1, 1)
        for t in (0, 2, 1, 3):
            h_ps[t] = psum.tile([P, HALF], F32, name="h_ps%d" % t, tag="bank%d" % t)
            second_product(h_ps[t][:], 1, t)
            if t == 2:
                nc.vector.tensor_scalar(h_win[t][:, HALF:], h_ps[t][:], 1.0 / 128, None, ALU.mult)
            else:
                nc.scalar.activation(h_win[t][:, HALF:], h_ps[t][:], ACT.Copy, scale=1.0 / 128)

        out_v = out_0.rearrange("(p t) j -> p t j", t=PACK)
        words_v = out_1[0].rearrange("p n t -> p (n t)").bitcast(I32)
        o_codes = held([P, S], U32, "o_codes")
        o_scales = held([P, S], U8, "o_scales")
        s = [held([P, PACK, HALF], F32, "s%d" % i) for i in range(2)]
        u = [held([P, PACK, HALF], F32, "u%d" % i) for i in range(2)]
        o = [held([P, PACK, HALF], F32, "o%d" % i) for i in range(2)]
        for i in range(2):
            for t in range(PACK):
                nc.scalar.activation(
                    s[i][:, t, :], h_win[t][:].indirect(cols(n4_t, i * HALF, HALF)), ACT.Sigmoid, scale=16.0
                )

        def tanh_times(out, sig, other):
            nc.vector.scalar_tensor_tensor(out, sig, half[:], other, ALU.subtract, ALU.mult)

        def place_times(out, t, c0, n, other):
            nc.vector.tensor_tensor(out, h_win[t][:].indirect(cols(n3_t, c0, n)), other, ALU.mult)

        def planes(i, src):
            quantize(o_codes, o_scales, src, i)
            c = slice(i * HALF, (i + 1) * HALF)
            nc.sync.dma_start(words_v[:, c], o_codes[:, c].bitcast(I32))

        for t in (0, 2, 1, 3):
            place_times(u[0][:, t, :], t, 0, HALF, h_plain[:, t, :])
        tanh_times(o[0][:], s[0][:], u[0][:])
        nc.sync.dma_start(out_v[:, :, :HALF], o[0][:])
        o_bf0 = held([P, HALF * PACK], BF16, "o_bf0")
        interleave(nc.scalar.copy, o_bf0[:], o[0][:])
        o_bf1 = held([P, HALF * PACK], BF16, "o_bf1")
        tanh_times(u[1][:, 0, :], s[1][:, 0, :], h_ps[0][:])
        for t in range(PACK - 1):
            tanh_times(u[1][:, t + 1, :], s[1][:, t + 1, :], h_ps[t + 1][:])
            place_times(o[1][:, t, :], t, HALF, HALF, u[1][:, t, :])
            nc.sync.dma_start(out_v[:, t, HALF:], o[1][:, t, :])
        place_times(o[1][:, 3, :QUARTER], 3, HALF, QUARTER, u[1][:, 3, :QUARTER])
        interleave(nc.scalar.copy, o_bf1[:, : QUARTER * PACK], o[1][:, :, :QUARTER])
        place_times(o[1][:, 3, QUARTER:], 3, HALF + QUARTER, QUARTER, u[1][:, 3, QUARTER:])
        nc.sync.dma_start(out_v[:, 3, HALF:], o[1][:, 3, :])
        planes(0, o_bf0)
        interleave(nc.vector.tensor_copy, o_bf1[:, QUARTER * PACK :], o[1][:, :, QUARTER:])
        planes(1, o_bf1)
        for r in range(4):
            queue = nc.scalar if r % 2 else nc.sync
            queue.dma_start(out_2[0][r:16:4, :].bitcast(I32), o_scales[r:P:32, :].bitcast(I32))
